import numpy as np
import ml_dtypes


def mxq(x, axis, fmt="e4m3"):
    dtype, down = {"e4m3": (ml_dtypes.float8_e4m3fn, 7), "e5m2": (ml_dtypes.float8_e5m2, 14)}[fmt]
    v = np.moveaxis(np.asarray(x, np.float32).astype(ml_dtypes.bfloat16).astype(np.float64), axis, -1)
    blocks = v.reshape(v.shape[:-1] + (-1, 32))
    amax = np.abs(blocks).max(-1, keepdims=True)
    byte = np.maximum(np.where(amax > 0, np.frexp(amax)[1] - 1 + 127, 0) - down, 1)
    scale = np.exp2(byte - 127.0)
    codes = (blocks / scale).astype(np.float32).astype(dtype).astype(np.float64)
    return np.moveaxis((codes * scale).reshape(v.shape), -1, axis)


WIDE = False


def mx_kscale(k):
    if not WIDE:
        return np.ones(k)
    levels = np.array([10, -10, 5, -5, 0])
    if k % 512:
        return np.exp2(np.random.permutation(np.resize(levels, k // 32))).repeat(32)
    a = np.empty((k // 512, 16))
    for p in range(k // 512):
        a[p, :8] = np.random.permutation(np.resize(levels, 8))
        for g in range(8):
            far = levels[np.abs(levels - a[p, g]) >= 10]
            a[p, g + 8] = far[np.random.randint(len(far))]
    return np.exp2(a.ravel()).repeat(32)


BF16 = ml_dtypes.bfloat16


def bf(x):
    return np.asarray(x, np.float32).astype(BF16)


def f64(x):
    return np.asarray(x).astype(np.float64)


E2M1 = np.array([0.0, 0.5, 1.0, 1.5, 2.0, 3.0, 4.0, 6.0, -0.0, -0.5, -1.0, -1.5, -2.0, -3.0, -4.0, -6.0])


def pack_weight(w, fmt):
    k, n = w.shape
    w = f64(bf(w)).reshape(k // 32, 32, n)
    amax = np.abs(w).max(1)
    if fmt == "e4m3":
        byte = np.frexp(amax)[1] - 1 + 127 - 7
    else:
        mant, ex = np.frexp(amax / 6.0)
        byte = np.where(mant > 0.5, ex, ex - 1) + 127
    byte = np.clip(np.where(amax > 0, byte, 1), 1, 254)
    scaled = (w * np.exp2(127.0 - byte)[:, None, :]).reshape(k, n).astype(np.float32)
    by_word = np.ascontiguousarray(scaled.reshape(k // 512, 128, 4, n).transpose(0, 1, 3, 2))
    if fmt == "e4m3":
        words = by_word.astype(ml_dtypes.float8_e4m3fn).view(np.uint8)
    else:
        c = by_word.astype(ml_dtypes.float4_e2m1fn).view(np.uint8) & 0xF
        words = c[..., 0::2] | (c[..., 1::2] << 4)
    return np.ascontiguousarray(words), np.ascontiguousarray(byte.astype(np.uint8).reshape(k // 512, 16, n))


def unpack_weight(words, scales, fmt):
    g, p, n, _ = words.shape
    if fmt == "e4m3":
        vals = np.ascontiguousarray(words).view(ml_dtypes.float8_e4m3fn).astype(np.float64)
    else:
        nib = np.empty((g, p, n, 4), np.uint8)
        nib[..., 0::2] = words & 0xF
        nib[..., 1::2] = words >> 4
        vals = E2M1[nib]
    vals = vals * np.repeat(np.exp2(scales.astype(np.float64) - 127.0), 8, axis=1)[..., None]
    return vals.transpose(0, 1, 3, 2).reshape(g * 512, n)
def pack4(w):
    words, scales = pack_weight(w, "e2m1")
    return words.reshape(words.shape[0], 128, -1), scales


def unpack4(words, scales):
    return unpack_weight(words.reshape(words.shape[0], 128, -1, 2), scales, "e2m1")


def planes(Y):
    n, m = Y.shape
    b = f64(bf(Y)).reshape(n // 32, 32, m)
    amax = np.abs(b).max(1)
    byte = np.clip(np.where(amax > 0, np.frexp(amax)[1] - 1 + 127 - 7, 1), 1, 254)
    codes = (b * np.exp2(127.0 - byte)[:, None, :]).reshape(n, m).astype(np.float32).astype(ml_dtypes.float8_e4m3fn).view(np.uint8)
    words = codes.reshape(n // 512, 128, 4, m).transpose(0, 1, 3, 2)
    return np.ascontiguousarray(words), np.ascontiguousarray(byte.astype(np.uint8).reshape(n // 512, 16, m))


R, CA, CB, F, Q = 1536, 512, 1024, 1024, 1024

def setup_inputs():
    sa, sb, t = mx_kscale(CA), mx_kscale(CB), mx_kscale(F)
    C = CA + CB
    stoich_a = np.random.randn(CA, R) * sa[:, None]
    stoich_b = np.random.randn(CB, R) * sb[:, None]
    moieties_a = np.random.randn(CA, F) / np.sqrt(C) / sa[:, None] * t
    moieties_b = np.random.randn(CB, F) / np.sqrt(C) / sb[:, None] * t
    mb_words, mb_scales = pack4(moieties_b)
    pair = 0.5 * np.random.randn(F) * t
    energies = 0.6 * np.random.randn(F, Q) / np.sqrt(F) / t[:, None]
    shift = 0.3 * np.random.randn(Q)
    rate_back = np.exp(0.8 * np.random.randn(R))
    return {"stoich_a": bf(stoich_a), "moieties_a": bf(moieties_a), "stoich_b": bf(stoich_b),
            "moieties_b_words": mb_words, "moieties_b_scales": mb_scales, "pair": bf(pair),
            "energies": bf(energies), "shift": bf(shift), "rate_back": bf(rate_back)}

def reference(stoich_a, moieties_a, stoich_b, moieties_b_words, moieties_b_scales, pair, energies, shift, rate_back):
    A = mxq(f64(stoich_a), 0, "e4m3")
    MA = mxq(f64(moieties_a), 0, "e4m3")
    B = mxq(f64(stoich_b), 0, "e4m3")
    MB = unpack4(moieties_b_words, moieties_b_scales)
    D = (A.T @ MA) + (B.T @ MB) + f64(pair)
    E = (mxq(D, 1, "e4m3") @ mxq(f64(energies), 0, "e4m3")) + f64(shift)
    y = f64(rate_back)[:, None] * np.exp(-E)
    Y = y
    words, scales = planes(Y)
    return y, words, scales

@@ -1,0 +1,313 @@
+from contextlib import ExitStack
+
+import concourse.mybir as mybir
+from concourse.masks import make_identity
+
+R, CA, CB, F, Q = 1536, 512, 1024, 1024, 1024
+FLOPS = 2 * R * F * (CA + CB) + 2 * R * Q * F
+
+F32 = mybir.dt.float32
+BF16 = mybir.dt.bfloat16
+I32 = mybir.dt.int32
+U32 = mybir.dt.uint32
+U8 = mybir.dt.uint8
+FP8X4 = mybir.dt.float8_e4m3fn_x4
+FP4X4 = mybir.dt.float4_e2m1fn_x4
+ALU = mybir.AluOpType
+ACT = mybir.ActivationFunctionType
+AX = mybir.AxisListType
+
+P = 128
+W = 512
+RUNS = W // 4
+G_RUNS = 80
+PLAN = """
+i:s00:72 i:s01:56 warm q:s00 mb q:s01 w:d00:0 w:d01:0 w:d00:1 w:d01:1 i:s02:64 i:m0:60 q:s02 sv i:m1:60 q:m0 sv2 w:d00:2 i:s10:60 q:m1 w:d01:2
+ i:s11:64 q:s10 i:s12:72 q:s11 x:d00 q:s12 n:d10 iv:e00:80 ig:d00:128 x:d01 n:d11 is:e00:80 q:d00
+ g:d01 z:d10 i:e10:0 q:e00 q:d10 q:d01 
+ g:e01 z:d11 q:e10 m:y00 i:e11:0 q:d11 m:y10 q:e01
+ g:s20 x:y00 q:e11 m:y01 q:s20
+ g:s21 x:y10 m:y11 q:s21
+ g:s22 x:y01 q:s22 n:d20
+ g:y00 x:y11 n:d21 q:y00
+ g:y10 z:d20 i:y01:0 q:d20 q:y10
+ g:y11 z:d21 q:y01 q:d21 m:y20 m:y21 q:y11
+ x:y20 
+ gg:y20:40 x:y21 vv:y20:40 is:y21:68 q:y20 iv:y21:68 q:y21
+"""
+
+
+def tile_reaction_gibbs_rates_k6_kernel(
+    tc, stoich_a, moieties_a, stoich_b, mb_words, mb_scales, pair, energies, shift, rate_back, out_0, out_1, out_2
+):
+    nc = tc.nc
+    with ExitStack() as ctx:
+        keep = ctx.enter_context(tc.tile_pool(name="keep", bufs=1))
+        work = ctx.enter_context(tc.tile_pool(name="work", bufs=3))
+        psum = ctx.enter_context(tc.psum_pool(name="psum", bufs=8))
+        ctx.enter_context(tc.manual_schedule())
+
+        raw = {}
+
+        def load_rows(name, rows):
+            t = keep.tile([P, 4, W], BF16, name="raw_" + name)
+            nc.sync.dma_start(out=t[:], in_=rows.rearrange("(p j) c -> p j c", j=4))
+            raw[name] = t[:]
+
+        def load_stoich(g, which):
+            cols = slice(W * g, W * (g + 1))
+            src = stoich_a[:, cols] if which == 2 else stoich_b[W * which : W * (which + 1), cols]
+            load_rows("s%d%d" % (g, which), src)
+
+        mbs_raw = keep.tile([P, 2, F], U8, name="mbs_raw")
+        nc.vector.memset(mbs_raw[:].bitcast(I32), 0)
+        ident = keep.tile([P, P], F32, name="ident")
+        make_identity(nc, ident[:])
+
+        rate = keep.tile([P, 3, 4], BF16, name="rate")
+        nc.sync.dma_start(out=rate[:], in_=rate_back.rearrange("(g p s) -> p g s", g=3, s=4))
+        load_stoich(0, 0)
+        load_stoich(0, 1)
+        mbw_raw = keep.tile([P, 2, 2 * F], U8, name="mbw_raw")
+        nc.sync.dma_start(out=mbw_raw[:].bitcast(I32), in_=mb_words.rearrange("k p n -> p k n").bitcast(I32))
+        for quad in range(4):
+            nc.sync.dma_start(
+                out=mbs_raw[32 * quad : 32 * quad + 4, :, :].bitcast(I32),
+                in_=mb_scales[:, 4 * quad : 4 * quad + 4, :].rearrange("k r n -> r k n").bitcast(I32),
+            )
+        load_stoich(0, 2)
+        load_rows("m0", moieties_a[:, 0:W])
+        load_rows("m1", moieties_a[:, W:F])
+        pair16 = keep.tile([P, 2, 16], BF16, name="pair16")
+        for k in range(2):
+            src = pair[W * k : W * (k + 1)].rearrange("(u e) -> u e", e=16)
+            nc.sync.dma_start(out=pair16[:, k, :], in_=src.unsqueeze(1).to_broadcast([32, 4, 16]))
+        for which in range(3):
+            load_stoich(1, which)
+        for k in range(2):
+            t = keep.tile([P, 4, Q], BF16, name="raw_e%d" % k)
+            rows = energies[W * k : W * (k + 1), :].rearrange("(u t b) q -> b u t q", t=4, b=4)
+            for b in range(4):
+                nc.sync.dma_start(out=t[b:P:4, :, :], in_=rows[b])
+            for h in range(2):
+                raw["e%d%d" % (k, h)] = t[:, :, W * h : W * (h + 1)]
+        shift_sb = keep.tile([P, Q], BF16, name="shift_sb")
+        nc.sync.dma_start(out=shift_sb[:], in_=shift.partition_broadcast(P))
+        for which in range(3):
+            load_stoich(2, which)
+
+        parts = keep.tile([P, 3, 12], F32, name="parts")
+        flat_rate = rate[:].rearrange("p g s -> p (g s)")
+        big = 2.0**64
+        nc.vector.tensor_scalar(parts[:, 0, :], flat_rate, big, 1.0 / big, ALU.min, ALU.max)
+        nc.vector.tensor_scalar(parts[:, 1, :], flat_rate, 1.0 / big, 1.0, ALU.mult, ALU.max)
+        nc.vector.tensor_scalar(parts[:, 2, :], flat_rate, big, 1.0, ALU.mult, ALU.min)
+        ln_parts = keep.tile([P, 3, 12], F32, name="ln_parts")
+        nc.scalar.activation(out=ln_parts[:], in_=parts[:], func=ACT.Ln)
+        lane = keep.tile([P, 4], F32, name="lane")
+        nc.vector.tensor_reduce(out=lane[:], in_=ident[:].rearrange("p (u b) -> p b u", b=4), axis=AX.X, op=ALU.add)
+
+        mbw = keep.tile([P, 2, 2 * F], U8, name="mbw", align_bytes=64)
+        mbs = keep.tile([P, 2, F], U8, name="mbs", align_bytes=64)
+        ln_rate = keep.tile([P, 12], F32, name="ln_rate")
+        pair_col = keep.tile([P, 8], F32, name="pair_col")
+
+        def order_moieties_b():
+            words_in = mbw_raw[:].rearrange("p k n -> p (k n)").bitcast(I32)
+            words_out = mbw[:].rearrange("p k n -> p (k n)").bitcast(I32)
+            nc.vector.tensor_copy(
+                out=words_out.rearrange("p (x t u e) -> p x t u e", t=4, u=32, e=2),
+                in_=words_in.rearrange("p (x u t e) -> p x t u e", t=4, u=32, e=2),
+            )
+            scales_in = mbs_raw[:].rearrange("p k n -> p (k n)").bitcast(I32)
+            scales_out = mbs[:].rearrange("p k n -> p (k n)").bitcast(I32)
+            nc.vector.tensor_copy(
+                out=scales_out.rearrange("p (x t u) -> p x t u", t=4, u=32),
+                in_=scales_in.rearrange("p (x u t) -> p x t u", t=4, u=32),
+            )
+
+        picked = keep.tile([P, 8, 4], F32, name="picked")
+
+        def small_vectors():
+            nc.vector.tensor_reduce(
+                out=ln_rate[:], in_=ln_parts[:].rearrange("p a c -> p c a"), axis=AX.X, op=ALU.add
+            )
+            nc.vector.tensor_tensor(
+                out=picked[:],
+                in0=pair16[:].rearrange("p k (t b) -> p (k t) b", b=4),
+                in1=lane[:].unsqueeze(1).to_broadcast([P, 8, 4]),
+                op=ALU.mult,
+            )
+
+        def small_vectors2():
+            nc.vector.tensor_reduce(out=pair_col[:], in_=picked[:], axis=AX.X, op=ALU.add)
+
+        codes, scales, banks, grouped = {}, {}, {}, {}
+        y_scales = [keep.tile([P, Q], U8, name="y_scales%d" % i, align_bytes=64) for i in range(2)]
+
+        def interleave(job, shares, tag="grouped"):
+            if job not in grouped:
+                grouped[job] = work.tile([P, 4 * W], BF16, name=tag, bufs=(4 if tag == "grouped" else 1), align_bytes=64)
+            if job[0] == "m":
+                dst = grouped[job][:].rearrange("p (t u b j) -> p u t j b", t=4, b=4, j=4)
+                src = raw[job].rearrange("p j (u t b) -> p u t j b", t=4, b=4)
+                unit = 4
+            else:
+                dst = grouped[job][:].rearrange("p (c i j) -> p c j i", i=4, j=4)
+                src = raw[job].rearrange("p j (c i) -> p c j i", i=4)
+                unit = 1
+            for engine, first, end in shares:
+                part = slice(first // unit, end // unit)
+                if first == end:
+                    continue
+                if engine == "v":
+                    nc.vector.tensor_copy(out=dst[:, part], in_=src[:, part])
+                elif engine == "s":
+                    nc.scalar.copy(out=dst[:, part], in_=src[:, part])
+                else:
+                    nc.gpsimd.tensor_scalar(dst[:, part], src[:, part], 1.0, 0.0, ALU.mult, ALU.add)
+
+        def quantize(job):
+            if job[0] == "y":
+                g, h = int(job[1]), int(job[2])
+                cols = slice(W * h, W * (h + 1))
+                words = work.tile([P, W], U32, name="y_words", align_bytes=64)
+                plane = y_scales[g // 2]
+                nc.vector.quantize_mx(out=words[:].bitcast(FP8X4), scales=plane[4 * (g % 2) :, cols], in_=grouped[job][:])
+                nc.sync.dma_start(
+                    out=out_1[g, :, cols, :].rearrange("p m t -> p (m t)").bitcast(I32), in_=words[:].bitcast(I32)
+                )
+                if h == 1 and g >= 1:
+                    groups = slice(0, 2) if g == 1 else slice(2, 3)
+                    rows = 8 if g == 1 else 4
+                    for quad in range(4):
+                        nc.sync.dma_start(
+                            out=out_2[groups, 4 * quad : 4 * quad + 4, :].bitcast(I32),
+                            in_=plane[32 * quad : 32 * quad + rows, :].bitcast(I32),
+                        )
+                return
+            codes[job] = keep.tile([P, W], U32, name="codes_" + job, align_bytes=64)
+            scales[job] = keep.tile([P, W], U8, name="scales_" + job, align_bytes=64)
+            nc.vector.quantize_mx(out=codes[job][:].bitcast(FP8X4), scales=scales[job][:], in_=grouped[job][:])
+
+        def stationary(job, slot, step):
+            g, h = int(job[1]), int(job[2])
+            cols = slice(P * slot, P * (slot + 1))
+            if job[0] == "y":
+                still = "d%d%d" % (g, step)
+                return codes[still][:, cols].bitcast(FP8X4), scales[still][:, cols]
+            if step == 2:
+                return codes["m%d" % h][:, cols].bitcast(FP8X4), scales["m%d" % h][:, cols]
+            first = W * h + P * slot
+            return mbw[:, step, 2 * first : 2 * (first + P)].bitcast(FP4X4), mbs[:, step, first : first + P]
+
+        def one_matmul(job, slot, step, out, cols):
+            g, h = int(job[1]), int(job[2])
+            moving, steps = ("e%d%d" % (step, h), 2) if job[0] == "y" else ("s%d%d" % (g, step), 3)
+            lhsT, lhsT_scale = stationary(job, slot, step)
+            nc.tensor.matmul_mx(
+                out=out,
+                lhsT=lhsT,
+                lhsT_scale=lhsT_scale,
+                rhs=codes[moving][:, cols].bitcast(FP8X4),
+                rhs_scale=scales[moving][:, cols],
+                start=(step == 0),
+                stop=(step == steps - 1),
+            )
+
+        def wide_pass(job, step):
+            for slot in range(4):
+                if step == 0:
+                    banks[job, slot] = psum.tile([P, W], F32, name="bank")
+                one_matmul(job, slot, step, banks[job, slot][:], slice(0, W))
+
+        def matmuls(job):
+            for slot in range(4):
+                banks[job, slot] = psum.tile([P, W], F32, name="bank")
+                for step in range(2 if job[0] == "y" else 3):
+                    one_matmul(job, slot, step, banks[job, slot][:], slice(0, W))
+
+        def narrow_matmuls(job):
+            for chunk in range(4):
+                banks[job, chunk] = psum.tile([P, W], F32, name="bank")
+                cols = slice(P * chunk, P * (chunk + 1))
+                for slot in range(4):
+                    for step in range(3):
+                        one_matmul(job, slot, step, banks[job, chunk][:, P * slot : P * (slot + 1)], cols)
+
+        def read_narrow(job):
+            h = int(job[2])
+            grouped[job] = work.tile([P, 4 * W], BF16, name="grouped", bufs=4, align_bytes=64)
+            dst = grouped[job][:].rearrange("p (s c m t) -> p c s m t", s=4, c=4, t=4)
+            bias = pair_col[:, 4 * h : 4 * h + 4].unsqueeze(1).unsqueeze(1).to_broadcast([P, 4, 32, 4])
+            for chunk in range(4):
+                src = banks[job, chunk][:].rearrange("p (t m s) -> p s m t", t=4, s=4)
+                nc.vector.tensor_tensor(out=dst[:, chunk], in0=src, in1=bias, op=ALU.add)
+
+        def read_banks(job):
+            g, h = int(job[1]), int(job[2])
+            if job[0] == "d":
+                t = work.tile([P, 4, W], BF16, name="d_rows", bufs=2)
+                for slot in range(4):
+                    nc.scalar.activation(
+                        out=t[:, slot, :].rearrange("p (s m) -> p s m", s=4),
+                        in_=banks[job, slot][:].rearrange("p (m s) -> p s m", s=4),
+                        func=ACT.Identity,
+                        bias=pair_col[:, 4 * h + slot : 4 * h + slot + 1],
+                    )
+            else:
+                t = work.tile([P, 4, W], F32, name="y_rows", bufs=4)
+                cols = slice(W * h, W * (h + 1))
+                rows = out_0[W * g : W * (g + 1), cols].rearrange("(p s) q -> p s q", s=4)
+                for slot in range(4):
+                    nc.vector.tensor_tensor(out=t[:, slot, :], in0=banks[job, slot][:], in1=shift_sb[:, cols], op=ALU.add)
+                    nc.scalar.activation(
+                        out=t[:, slot, :],
+                        in_=t[:, slot, :],
+                        func=ACT.Exp,
+                        bias=ln_rate[:, 4 * g + slot : 4 * g + slot + 1],
+                        scale=-1.0,
+                    )
+                    nc.sync.dma_start(out=rows[:, slot, :], in_=t[:, slot, :])
+            raw[job] = t[:]
+
+        for item in PLAN.split():
+            op, job, arg = (item.split(":") + ["", ""])[:3]
+            if op == "i":
+                interleave(job, [("v", 0, int(arg)), ("s", int(arg), RUNS)])
+            elif op == "iv":
+                interleave(job, [("v", 0, int(arg))])
+            elif op == "is":
+                interleave(job, [("s", int(arg), RUNS)])
+            elif op == "g":
+                cut = int(arg) if arg else G_RUNS
+                interleave(job, [("g", 0, cut), ("s", cut, RUNS)], tag="for_gpsimd")
+            elif op == "q":
+                quantize(job)
+            elif op == "w":
+                wide_pass(job, int(arg))
+            elif op == "m":
+                matmuls(job)
+            elif op == "n":
+                narrow_matmuls(job)
+            elif op == "x":
+                read_banks(job)
+            elif op == "z":
+                read_narrow(job)
+            elif op == "warm":
+                warm = keep.tile([P, 1], F32, name="warm")
+                nc.scalar.activation(out=warm[:], in_=ln_parts[:, 0, 0:1], func=ACT.Exp)
+            elif op == "mb":
+                order_moieties_b()
+            elif op == "sv2":
+                small_vectors2()
+            elif op == "ig":
+                interleave(job, [("v", 0, int(arg)), ("s", int(arg), RUNS)], tag="for_gpsimd")
+            elif op == "gv":
+                interleave(job, [("g", 0, int(arg)), ("v", int(arg), RUNS)], tag="for_gpsimd")
+            elif op == "gg":
+                interleave(job, [("g", 0, int(arg))], tag="for_gpsimd")
+            elif op == "vv":
+                interleave(job, [("v", int(arg), RUNS)])
+            elif op == "sv":
+                small_vectors()

@@ -20,20 +20,20 @@ AX = mybir.AxisListType
 P = 128
 W = 512
 RUNS = W // 4
-G_RUNS = 80
+G_RUNS = 88
+EARLY_A = 0
 PLAN = """
-i:s00:72 i:s01:56 warm q:s00 mb q:s01 w:d00:0 w:d01:0 w:d00:1 w:d01:1 i:s02:64 i:m0:60 q:s02 sv i:m1:60 q:m0 sv2 w:d00:2 i:s10:60 q:m1 w:d01:2
- i:s11:64 q:s10 i:s12:72 q:s11 x:d00 q:s12 n:d10 iv:e00:80 ig:d00:128 x:d01 n:d11 is:e00:80 q:d00
- g:d01 z:d10 i:e10:0 q:e00 q:d10 q:d01 
- g:e01 z:d11 q:e10 m:y00 i:e11:0 q:d11 m:y10 q:e01
- g:s20 x:y00 q:e11 m:y01 q:s20
- g:s21 x:y10 m:y11 q:s21
- g:s22 x:y01 q:s22 n:d20
- g:y00 x:y11 n:d21 q:y00
- g:y10 z:d20 i:y01:0 q:d20 q:y10
- g:y11 z:d21 q:y01 q:d21 m:y20 m:y21 q:y11
- x:y20 
- gg:y20:40 x:y21 vv:y20:40 is:y21:68 q:y20 iv:y21:68 q:y21
+warm i:s00:128 i:s01:40 q:s00 mb q:s01 w:d00:0 w:d01:0 w:d00:1 w:d01:1 i:s02:56 i:m0:60 q:s02 sv i:m1:60 q:m0 sv2 w:d00:2 i:s10:60 q:m1 w:d01:2
+ i:s11:64 q:s10 i:s12:72 q:s11 x:d00 q:s12 n:d10 i:e00:128 x:d01 n:d11 ig:d00:128 q:d00 q:e00 
+ g:e10 z:d10 i:d01:0 i:s20:0 q:d10 q:e10 q:d01 m:y00
+ g:s21 z:d11 i:s22:0 q:d11 m:y10 q:s20 q:s21 q:s22 m:d20
+ g:e01 x:y00 q:e01
+ g:e11 x:y10 n:d21 x:d20 q:e11 m:y01
+ gg:y00:120 r:y00:s,120,128 z:d21 m:y11 i:y10:0 q:d21 q:y00
+ g:d20 x:y01 q:y10 q:d20 m:y20 
+ gg:y01:128 x:y11 m:y21 
+ g2:y11:128 x:y20 
+ x:y21:2 q:y01 r:y20:v,0,64 st:y21:2 q:y11 r:y20:v,64,128 st:y21:3 r:y21:s,0,88 q:y20 r:y21:v,88,128 qa:y21 qb:y21
 """
 
 
@@ -68,6 +68,8 @@ def tile_reaction_gibbs_rates_k6_kernel(
         nc.sync.dma_start(out=rate[:], in_=rate_back.rearrange("(g p s) -> p g s", g=3, s=4))
         load_stoich(0, 0)
         load_stoich(0, 1)
+        if EARLY_A:
+            load_stoich(0, 2)
         mbw_raw = keep.tile([P, 2, 2 * F], U8, name="mbw_raw")
         nc.sync.dma_start(out=mbw_raw[:].bitcast(I32), in_=mb_words.rearrange("k p n -> p k n").bitcast(I32))
         for quad in range(4):
@@ -75,7 +77,8 @@ def tile_reaction_gibbs_rates_k6_kernel(
                 out=mbs_raw[32 * quad : 32 * quad + 4, :, :].bitcast(I32),
                 in_=mb_scales[:, 4 * quad : 4 * quad + 4, :].rearrange("k r n -> r k n").bitcast(I32),
             )
-        load_stoich(0, 2)
+        if not EARLY_A:
+            load_stoich(0, 2)
         load_rows("m0", moieties_a[:, 0:W])
         load_rows("m1", moieties_a[:, W:F])
         pair16 = keep.tile([P, 2, 16], BF16, name="pair16")
@@ -167,21 +170,31 @@ def tile_reaction_gibbs_rates_k6_kernel(
                 else:
                     nc.gpsimd.tensor_scalar(dst[:, part], src[:, part], 1.0, 0.0, ALU.mult, ALU.add)
 
-        def quantize(job):
+        y_words = {}
+
+        def quantize(job, first=0, end=W):
             if job[0] == "y":
                 g, h = int(job[1]), int(job[2])
-                cols = slice(W * h, W * (h + 1))
-                words = work.tile([P, W], U32, name="y_words", align_bytes=64)
-                plane = y_scales[g // 2]
-                nc.vector.quantize_mx(out=words[:].bitcast(FP8X4), scales=plane[4 * (g % 2) :, cols], in_=grouped[job][:])
-                nc.sync.dma_start(
-                    out=out_1[g, :, cols, :].rearrange("p m t -> p (m t)").bitcast(I32), in_=words[:].bitcast(I32)
+                if first == 0:
+                    y_words[job] = work.tile([P, W], U32, name="y_words", bufs=4, align_bytes=64)
+                words = y_words[job]
+                plane = y_scales[min(g, 1)]
+                nc.vector.quantize_mx(
+                    out=words[:, first:end].bitcast(FP8X4),
+                    scales=plane[4 * (g // 2) :, W * h + first : W * h + end],
+                    in_=grouped[job][:, 4 * first : 4 * end],
                 )
-                if h == 1 and g >= 1:
-                    groups = slice(0, 2) if g == 1 else slice(2, 3)
-                    rows = 8 if g == 1 else 4
+                if end < W:
+                    return
+                nc.sync.dma_start(
+                    out=out_1[g, :, W * h : W * (h + 1), :].rearrange("p m t -> p (m t)").bitcast(I32),
+                    in_=words[:].bitcast(I32),
+                )
+                if h == 1 and g != 1:
+                    groups = slice(0, 1) if g == 0 else slice(1, 3)
+                    rows = 4 if g == 0 else 8
                     for quad in range(4):
-                        nc.sync.dma_start(
+                        (nc.sync if g == 0 else nc.scalar).dma_start(
                             out=out_2[groups, 4 * quad : 4 * quad + 4, :].bitcast(I32),
                             in_=plane[32 * quad : 32 * quad + rows, :].bitcast(I32),
                         )
@@ -244,7 +257,9 @@ def tile_reaction_gibbs_rates_k6_kernel(
                 src = banks[job, chunk][:].rearrange("p (t m s) -> p s m t", t=4, s=4)
                 nc.vector.tensor_tensor(out=dst[:, chunk], in0=src, in1=bias, op=ALU.add)
 
-        def read_banks(job):
+        late = {}
+
+        def read_banks(job, held=4):
             g, h = int(job[1]), int(job[2])
             if job[0] == "d":
                 t = work.tile([P, 4, W], BF16, name="d_rows", bufs=2)
@@ -268,7 +283,9 @@ def tile_reaction_gibbs_rates_k6_kernel(
                         bias=ln_rate[:, 4 * g + slot : 4 * g + slot + 1],
                         scale=-1.0,
                     )
-                    nc.sync.dma_start(out=rows[:, slot, :], in_=t[:, slot, :])
+                    if slot < held:
+                        nc.sync.dma_start(out=rows[:, slot, :], in_=t[:, slot, :])
+                late[job] = (rows, t)
             raw[job] = t[:]
 
         for item in PLAN.split():
@@ -291,7 +308,9 @@ def tile_reaction_gibbs_rates_k6_kernel(
             elif op == "n":
                 narrow_matmuls(job)
             elif op == "x":
-                read_banks(job)
+                read_banks(job, int(arg) if arg else 4)
+            elif op == "st":
+                nc.sync.dma_start(out=late[job][0][:, int(arg), :], in_=late[job][1][:, int(arg), :])
             elif op == "z":
                 read_narrow(job)
             elif op == "warm":
@@ -305,9 +324,18 @@ def tile_reaction_gibbs_rates_k6_kernel(
                 interleave(job, [("v", 0, int(arg)), ("s", int(arg), RUNS)], tag="for_gpsimd")
             elif op == "gv":
                 interleave(job, [("g", 0, int(arg)), ("v", int(arg), RUNS)], tag="for_gpsimd")
+            elif op == "g2":
+                interleave(job, [("g", 0, int(arg))], tag="for_gpsimd2")
             elif op == "gg":
                 interleave(job, [("g", 0, int(arg))], tag="for_gpsimd")
             elif op == "vv":
                 interleave(job, [("v", int(arg), RUNS)])
+            elif op == "r":
+                e, a, b = arg.split(",")
+                interleave(job, [(e, int(a), int(b))])
+            elif op == "qa":
+                quantize(job, 0, W // 2)
+            elif op == "qb":
+                quantize(job, W // 2, W)
             elif op == "sv":
                 small_vectors()

from contextlib import ExitStack

import concourse.mybir as mybir
from concourse.masks import make_identity

R, CA, CB, F, Q = 1536, 512, 1024, 1024, 1024
FLOPS = 2 * R * F * (CA + CB) + 2 * R * Q * F

F32 = mybir.dt.float32
BF16 = mybir.dt.bfloat16
I32 = mybir.dt.int32
U32 = mybir.dt.uint32
U8 = mybir.dt.uint8
FP8X4 = mybir.dt.float8_e4m3fn_x4
FP4X4 = mybir.dt.float4_e2m1fn_x4
ALU = mybir.AluOpType
ACT = mybir.ActivationFunctionType
AX = mybir.AxisListType

P = 128
W = 512
RUNS = W // 4
G_RUNS = 88
EARLY_A = 0
PLAN = """
warm i:s00:128 i:s01:40 q:s00 mb q:s01 w:d00:0 w:d01:0 w:d00:1 w:d01:1 i:s02:56 i:m0:60 q:s02 sv i:m1:60 q:m0 sv2 w:d00:2 i:s10:60 q:m1 w:d01:2
 i:s11:64 q:s10 i:s12:72 q:s11 x:d00 q:s12 n:d10 i:e00:128 x:d01 n:d11 ig:d00:128 q:d00 q:e00 
 g:e10 z:d10 i:d01:0 i:s20:0 q:d10 q:e10 q:d01 m:y00
 g:s21 z:d11 i:s22:0 q:d11 m:y10 q:s20 q:s21 q:s22 m:d20
 g:e01 x:y00 q:e01
 g:e11 x:y10 n:d21 x:d20 q:e11 m:y01
 gg:y00:120 r:y00:s,120,128 z:d21 m:y11 i:y10:0 q:d21 q:y00
 g:d20 x:y01 q:y10 q:d20 m:y20 
 gg:y01:128 x:y11 m:y21 
 g2:y11:128 x:y20 
 x:y21:2 q:y01 r:y20:v,0,64 st:y21:2 q:y11 r:y20:v,64,128 st:y21:3 r:y21:s,0,88 q:y20 r:y21:v,88,128 qa:y21 qb:y21
"""


def tile_reaction_gibbs_rates_k6_kernel(
    tc, stoich_a, moieties_a, stoich_b, mb_words, mb_scales, pair, energies, shift, rate_back, out_0, out_1, out_2
):
    nc = tc.nc
    with ExitStack() as ctx:
        keep = ctx.enter_context(tc.tile_pool(name="keep", bufs=1))
        work = ctx.enter_context(tc.tile_pool(name="work", bufs=3))
        psum = ctx.enter_context(tc.psum_pool(name="psum", bufs=8))
        ctx.enter_context(tc.manual_schedule())

        raw = {}

        def load_rows(name, rows):
            t = keep.tile([P, 4, W], BF16, name="raw_" + name)
            nc.sync.dma_start(out=t[:], in_=rows.rearrange("(p j) c -> p j c", j=4))
            raw[name] = t[:]

        def load_stoich(g, which):
            cols = slice(W * g, W * (g + 1))
            src = stoich_a[:, cols] if which == 2 else stoich_b[W * which : W * (which + 1), cols]
            load_rows("s%d%d" % (g, which), src)

        mbs_raw = keep.tile([P, 2, F], U8, name="mbs_raw")
        nc.vector.memset(mbs_raw[:].bitcast(I32), 0)
        ident = keep.tile([P, P], F32, name="ident")
        make_identity(nc, ident[:])

        rate = keep.tile([P, 3, 4], BF16, name="rate")
        nc.sync.dma_start(out=rate[:], in_=rate_back.rearrange("(g p s) -> p g s", g=3, s=4))
        load_stoich(0, 0)
        load_stoich(0, 1)
        if EARLY_A:
            load_stoich(0, 2)
        mbw_raw = keep.tile([P, 2, 2 * F], U8, name="mbw_raw")
        nc.sync.dma_start(out=mbw_raw[:].bitcast(I32), in_=mb_words.rearrange("k p n -> p k n").bitcast(I32))
        for quad in range(4):
            nc.sync.dma_start(
                out=mbs_raw[32 * quad : 32 * quad + 4, :, :].bitcast(I32),
                in_=mb_scales[:, 4 * quad : 4 * quad + 4, :].rearrange("k r n -> r k n").bitcast(I32),
            )
        if not EARLY_A:
            load_stoich(0, 2)
        load_rows("m0", moieties_a[:, 0:W])
        load_rows("m1", moieties_a[:, W:F])
        pair16 = keep.tile([P, 2, 16], BF16, name="pair16")
        for k in range(2):
            src = pair[W * k : W * (k + 1)].rearrange("(u e) -> u e", e=16)
            nc.sync.dma_start(out=pair16[:, k, :], in_=src.unsqueeze(1).to_broadcast([32, 4, 16]))
        for which in range(3):
            load_stoich(1, which)
        for k in range(2):
            t = keep.tile([P, 4, Q], BF16, name="raw_e%d" % k)
            rows = energies[W * k : W * (k + 1), :].rearrange("(u t b) q -> b u t q", t=4, b=4)
            for b in range(4):
                nc.sync.dma_start(out=t[b:P:4, :, :], in_=rows[b])
            for h in range(2):
                raw["e%d%d" % (k, h)] = t[:, :, W * h : W * (h + 1)]
        shift_sb = keep.tile([P, Q], BF16, name="shift_sb")
        nc.sync.dma_start(out=shift_sb[:], in_=shift.partition_broadcast(P))
        for which in range(3):
            load_stoich(2, which)

        parts = keep.tile([P, 3, 12], F32, name="parts")
        flat_rate = rate[:].rearrange("p g s -> p (g s)")
        big = 2.0**64
        nc.vector.tensor_scalar(parts[:, 0, :], flat_rate, big, 1.0 / big, ALU.min, ALU.max)
        nc.vector.tensor_scalar(parts[:, 1, :], flat_rate, 1.0 / big, 1.0, ALU.mult, ALU.max)
        nc.vector.tensor_scalar(parts[:, 2, :], flat_rate, big, 1.0, ALU.mult, ALU.min)
        ln_parts = keep.tile([P, 3, 12], F32, name="ln_parts")
        nc.scalar.activation(out=ln_parts[:], in_=parts[:], func=ACT.Ln)
        lane = keep.tile([P, 4], F32, name="lane")
        nc.vector.tensor_reduce(out=lane[:], in_=ident[:].rearrange("p (u b) -> p b u", b=4), axis=AX.X, op=ALU.add)

        mbw = keep.tile([P, 2, 2 * F], U8, name="mbw", align_bytes=64)
        mbs = keep.tile([P, 2, F], U8, name="mbs", align_bytes=64)
        ln_rate = keep.tile([P, 12], F32, name="ln_rate")
        pair_col = keep.tile([P, 8], F32, name="pair_col")

        def order_moieties_b():
            words_in = mbw_raw[:].rearrange("p k n -> p (k n)").bitcast(I32)
            words_out = mbw[:].rearrange("p k n -> p (k n)").bitcast(I32)
            nc.vector.tensor_copy(
                out=words_out.rearrange("p (x t u e) -> p x t u e", t=4, u=32, e=2),
                in_=words_in.rearrange("p (x u t e) -> p x t u e", t=4, u=32, e=2),
            )
            scales_in = mbs_raw[:].rearrange("p k n -> p (k n)").bitcast(I32)
            scales_out = mbs[:].rearrange("p k n -> p (k n)").bitcast(I32)
            nc.vector.tensor_copy(
                out=scales_out.rearrange("p (x t u) -> p x t u", t=4, u=32),
                in_=scales_in.rearrange("p (x u t) -> p x t u", t=4, u=32),
            )

        picked = keep.tile([P, 8, 4], F32, name="picked")

        def small_vectors():
            nc.vector.tensor_reduce(
                out=ln_rate[:], in_=ln_parts[:].rearrange("p a c -> p c a"), axis=AX.X, op=ALU.add
            )
            nc.vector.tensor_tensor(
                out=picked[:],
                in0=pair16[:].rearrange("p k (t b) -> p (k t) b", b=4),
                in1=lane[:].unsqueeze(1).to_broadcast([P, 8, 4]),
                op=ALU.mult,
            )

        def small_vectors2():
            nc.vector.tensor_reduce(out=pair_col[:], in_=picked[:], axis=AX.X, op=ALU.add)

        codes, scales, banks, grouped = {}, {}, {}, {}
        y_scales = [keep.tile([P, Q], U8, name="y_scales%d" % i, align_bytes=64) for i in range(2)]

        def interleave(job, shares, tag="grouped"):
            if job not in grouped:
                grouped[job] = work.tile([P, 4 * W], BF16, name=tag, bufs=(4 if tag == "grouped" else 1), align_bytes=64)
            if job[0] == "m":
                dst = grouped[job][:].rearrange("p (t u b j) -> p u t j b", t=4, b=4, j=4)
                src = raw[job].rearrange("p j (u t b) -> p u t j b", t=4, b=4)
                unit = 4
            else:
                dst = grouped[job][:].rearrange("p (c i j) -> p c j i", i=4, j=4)
                src = raw[job].rearrange("p j (c i) -> p c j i", i=4)
                unit = 1
            for engine, first, end in shares:
                part = slice(first // unit, end // unit)
                if first == end:
                    continue
                if engine == "v":
                    nc.vector.tensor_copy(out=dst[:, part], in_=src[:, part])
                elif engine == "s":
                    nc.scalar.copy(out=dst[:, part], in_=src[:, part])
                else:
                    nc.gpsimd.tensor_scalar(dst[:, part], src[:, part], 1.0, 0.0, ALU.mult, ALU.add)

        y_words = {}

        def quantize(job, first=0, end=W):
            if job[0] == "y":
                g, h = int(job[1]), int(job[2])
                if first == 0:
                    y_words[job] = work.tile([P, W], U32, name="y_words", bufs=4, align_bytes=64)
                words = y_words[job]
                plane = y_scales[min(g, 1)]
                nc.vector.quantize_mx(
                    out=words[:, first:end].bitcast(FP8X4),
                    scales=plane[4 * (g // 2) :, W * h + first : W * h + end],
                    in_=grouped[job][:, 4 * first : 4 * end],
                )
                if end < W:
                    return
                nc.sync.dma_start(
                    out=out_1[g, :, W * h : W * (h + 1), :].rearrange("p m t -> p (m t)").bitcast(I32),
                    in_=words[:].bitcast(I32),
                )
                if h == 1 and g != 1:
                    groups = slice(0, 1) if g == 0 else slice(1, 3)
                    rows = 4 if g == 0 else 8
                    for quad in range(4):
                        (nc.sync if g == 0 else nc.scalar).dma_start(
                            out=out_2[groups, 4 * quad : 4 * quad + 4, :].bitcast(I32),
                            in_=plane[32 * quad : 32 * quad + rows, :].bitcast(I32),
                        )
                return
            codes[job] = keep.tile([P, W], U32, name="codes_" + job, align_bytes=64)
            scales[job] = keep.tile([P, W], U8, name="scales_" + job, align_bytes=64)
            nc.vector.quantize_mx(out=codes[job][:].bitcast(FP8X4), scales=scales[job][:], in_=grouped[job][:])

        def stationary(job, slot, step):
            g, h = int(job[1]), int(job[2])
            cols = slice(P * slot, P * (slot + 1))
            if job[0] == "y":
                still = "d%d%d" % (g, step)
                return codes[still][:, cols].bitcast(FP8X4), scales[still][:, cols]
            if step == 2:
                return codes["m%d" % h][:, cols].bitcast(FP8X4), scales["m%d" % h][:, cols]
            first = W * h + P * slot
            return mbw[:, step, 2 * first : 2 * (first + P)].bitcast(FP4X4), mbs[:, step, first : first + P]

        def one_matmul(job, slot, step, out, cols):
            g, h = int(job[1]), int(job[2])
            moving, steps = ("e%d%d" % (step, h), 2) if job[0] == "y" else ("s%d%d" % (g, step), 3)
            lhsT, lhsT_scale = stationary(job, slot, step)
            nc.tensor.matmul_mx(
                out=out,
                lhsT=lhsT,
                lhsT_scale=lhsT_scale,
                rhs=codes[moving][:, cols].bitcast(FP8X4),
                rhs_scale=scales[moving][:, cols],
                start=(step == 0),
                stop=(step == steps - 1),
            )

        def wide_pass(job, step):
            for slot in range(4):
                if step == 0:
                    banks[job, slot] = psum.tile([P, W], F32, name="bank")
                one_matmul(job, slot, step, banks[job, slot][:], slice(0, W))

        def matmuls(job):
            for slot in range(4):
                banks[job, slot] = psum.tile([P, W], F32, name="bank")
                for step in range(2 if job[0] == "y" else 3):
                    one_matmul(job, slot, step, banks[job, slot][:], slice(0, W))

        def narrow_matmuls(job):
            for chunk in range(4):
                banks[job, chunk] = psum.tile([P, W], F32, name="bank")
                cols = slice(P * chunk, P * (chunk + 1))
                for slot in range(4):
                    for step in range(3):
                        one_matmul(job, slot, step, banks[job, chunk][:, P * slot : P * (slot + 1)], cols)

        def read_narrow(job):
            h = int(job[2])
            grouped[job] = work.tile([P, 4 * W], BF16, name="grouped", bufs=4, align_bytes=64)
            dst = grouped[job][:].rearrange("p (s c m t) -> p c s m t", s=4, c=4, t=4)
            bias = pair_col[:, 4 * h : 4 * h + 4].unsqueeze(1).unsqueeze(1).to_broadcast([P, 4, 32, 4])
            for chunk in range(4):
                src = banks[job, chunk][:].rearrange("p (t m s) -> p s m t", t=4, s=4)
                nc.vector.tensor_tensor(out=dst[:, chunk], in0=src, in1=bias, op=ALU.add)

        late = {}

        def read_banks(job, held=4):
            g, h = int(job[1]), int(job[2])
            if job[0] == "d":
                t = work.tile([P, 4, W], BF16, name="d_rows", bufs=2)
                for slot in range(4):
                    nc.scalar.activation(
                        out=t[:, slot, :].rearrange("p (s m) -> p s m", s=4),
                        in_=banks[job, slot][:].rearrange("p (m s) -> p s m", s=4),
                        func=ACT.Identity,
                        bias=pair_col[:, 4 * h + slot : 4 * h + slot + 1],
                    )
            else:
                t = work.tile([P, 4, W], F32, name="y_rows", bufs=4)
                cols = slice(W * h, W * (h + 1))
                rows = out_0[W * g : W * (g + 1), cols].rearrange("(p s) q -> p s q", s=4)
                for slot in range(4):
                    nc.vector.tensor_tensor(out=t[:, slot, :], in0=banks[job, slot][:], in1=shift_sb[:, cols], op=ALU.add)
                    nc.scalar.activation(
                        out=t[:, slot, :],
                        in_=t[:, slot, :],
                        func=ACT.Exp,
                        bias=ln_rate[:, 4 * g + slot : 4 * g + slot + 1],
                        scale=-1.0,
                    )
                    if slot < held:
                        nc.sync.dma_start(out=rows[:, slot, :], in_=t[:, slot, :])
                late[job] = (rows, t)
            raw[job] = t[:]

        for item in PLAN.split():
            op, job, arg = (item.split(":") + ["", ""])[:3]
            if op == "i":
                interleave(job, [("v", 0, int(arg)), ("s", int(arg), RUNS)])
            elif op == "iv":
                interleave(job, [("v", 0, int(arg))])
            elif op == "is":
                interleave(job, [("s", int(arg), RUNS)])
            elif op == "g":
                cut = int(arg) if arg else G_RUNS
                interleave(job, [("g", 0, cut), ("s", cut, RUNS)], tag="for_gpsimd")
            elif op == "q":
                quantize(job)
            elif op == "w":
                wide_pass(job, int(arg))
            elif op == "m":
                matmuls(job)
            elif op == "n":
                narrow_matmuls(job)
            elif op == "x":
                read_banks(job, int(arg) if arg else 4)
            elif op == "st":
                nc.sync.dma_start(out=late[job][0][:, int(arg), :], in_=late[job][1][:, int(arg), :])
            elif op == "z":
                read_narrow(job)
            elif op == "warm":
                warm = keep.tile([P, 1], F32, name="warm")
                nc.scalar.activation(out=warm[:], in_=ln_parts[:, 0, 0:1], func=ACT.Exp)
            elif op == "mb":
                order_moieties_b()
            elif op == "sv2":
                small_vectors2()
            elif op == "ig":
                interleave(job, [("v", 0, int(arg)), ("s", int(arg), RUNS)], tag="for_gpsimd")
            elif op == "gv":
                interleave(job, [("g", 0, int(arg)), ("v", int(arg), RUNS)], tag="for_gpsimd")
            elif op == "g2":
                interleave(job, [("g", 0, int(arg))], tag="for_gpsimd2")
            elif op == "gg":
                interleave(job, [("g", 0, int(arg))], tag="for_gpsimd")
            elif op == "vv":
                interleave(job, [("v", int(arg), RUNS)])
            elif op == "r":
                e, a, b = arg.split(",")
                interleave(job, [(e, int(a), int(b))])
            elif op == "qa":
                quantize(job, 0, W // 2)
            elif op == "qb":
                quantize(job, W // 2, W)
            elif op == "sv":
                small_vectors()
